import numpy as np
import ml_dtypes


def mxq(x, axis, fmt="e4m3"):
    dtype, down = {"e4m3": (ml_dtypes.float8_e4m3fn, 7), "e5m2": (ml_dtypes.float8_e5m2, 14)}[fmt]
    v = np.moveaxis(np.asarray(x, np.float32).astype(ml_dtypes.bfloat16).astype(np.float64), axis, -1)
    blocks = v.reshape(v.shape[:-1] + (-1, 32))
    amax = np.abs(blocks).max(-1, keepdims=True)
    byte = np.maximum(np.where(amax > 0, np.frexp(amax)[1] - 1 + 127, 0) - down, 1)
    scale = np.exp2(byte - 127.0)
    codes = (blocks / scale).astype(np.float32).astype(dtype).astype(np.float64)
    return np.moveaxis((codes * scale).reshape(v.shape), -1, axis)


WIDE = False


def mx_kscale(k):
    if not WIDE:
        return np.ones(k)
    levels = np.array([10, -10, 5, -5, 0])
    if k % 512:
        return np.exp2(np.random.permutation(np.resize(levels, k // 32))).repeat(32)
    a = np.empty((k // 512, 16))
    for p in range(k // 512):
        a[p, :8] = np.random.permutation(np.resize(levels, 8))
        for g in range(8):
            far = levels[np.abs(levels - a[p, g]) >= 10]
            a[p, g + 8] = far[np.random.randint(len(far))]
    return np.exp2(a.ravel()).repeat(32)


BF16 = ml_dtypes.bfloat16


def bf(x):
    return np.asarray(x, np.float32).astype(BF16)


def f64(x):
    return np.asarray(x).astype(np.float64)


E2M1 = np.array([0.0, 0.5, 1.0, 1.5, 2.0, 3.0, 4.0, 6.0, -0.0, -0.5, -1.0, -1.5, -2.0, -3.0, -4.0, -6.0])


def pack_weight(w, fmt):
    k, n = w.shape
    w = f64(bf(w)).reshape(k // 32, 32, n)
    amax = np.abs(w).max(1)
    if fmt == "e4m3":
        byte = np.frexp(amax)[1] - 1 + 127 - 7
    else:
        mant, ex = np.frexp(amax / 6.0)
        byte = np.where(mant > 0.5, ex, ex - 1) + 127
    byte = np.clip(np.where(amax > 0, byte, 1), 1, 254)
    scaled = (w * np.exp2(127.0 - byte)[:, None, :]).reshape(k, n).astype(np.float32)
    by_word = np.ascontiguousarray(scaled.reshape(k // 512, 128, 4, n).transpose(0, 1, 3, 2))
    if fmt == "e4m3":
        words = by_word.astype(ml_dtypes.float8_e4m3fn).view(np.uint8)
    else:
        c = by_word.astype(ml_dtypes.float4_e2m1fn).view(np.uint8) & 0xF
        words = c[..., 0::2] | (c[..., 1::2] << 4)
    return np.ascontiguousarray(words), np.ascontiguousarray(byte.astype(np.uint8).reshape(k // 512, 16, n))


def unpack_weight(words, scales, fmt):
    g, p, n, _ = words.shape
    if fmt == "e4m3":
        vals = np.ascontiguousarray(words).view(ml_dtypes.float8_e4m3fn).astype(np.float64)
    else:
        nib = np.empty((g, p, n, 4), np.uint8)
        nib[..., 0::2] = words & 0xF
        nib[..., 1::2] = words >> 4
        vals = E2M1[nib]
    vals = vals * np.repeat(np.exp2(scales.astype(np.float64) - 127.0), 8, axis=1)[..., None]
    return vals.transpose(0, 1, 3, 2).reshape(g * 512, n)
def pack4(w):
    words, scales = pack_weight(w, "e2m1")
    return words.reshape(words.shape[0], 128, -1), scales


def unpack4(words, scales):
    return unpack_weight(words.reshape(words.shape[0], 128, -1, 2), scales, "e2m1")


def planes(Y):
    n, m = Y.shape
    b = f64(bf(Y)).reshape(n // 32, 32, m)
    amax = np.abs(b).max(1)
    byte = np.clip(np.where(amax > 0, np.frexp(amax)[1] - 1 + 127 - 7, 1), 1, 254)
    codes = (b * np.exp2(127.0 - byte)[:, None, :]).reshape(n, m).astype(np.float32).astype(ml_dtypes.float8_e4m3fn).view(np.uint8)
    words = codes.reshape(n // 512, 128, 4, m).transpose(0, 1, 3, 2)
    return np.ascontiguousarray(words), np.ascontiguousarray(byte.astype(np.uint8).reshape(n // 512, 16, m))


P, I, F, N = 1280, 2048, 1024, 1536


def setup_inputs():
    s = mx_kscale(I)
    t = mx_kscale(F)
    responses = bf(np.random.randn(P, I) * s[None, :])
    a_words, a_scales = pack4(np.random.randn(I, F) / np.sqrt(I) / s[:, None])
    half_width = bf(1.5 * np.exp(0.3 * np.random.randn(F)) * t)
    v_words, v_scales = pack4(np.random.randn(F, N) / np.sqrt(F) / t[:, None])
    sd = np.exp(0.8 * np.random.randn(N))
    prior_sd = bf(sd)
    prior_mean = bf(0.3 * sd * np.random.randn(N))
    reliability = bf(1.0 / (1.0 + np.exp(-1.0 - np.random.randn(P))))
    return {"responses": responses, "a_words": a_words, "a_scales": a_scales,
            "half_width": half_width, "v_words": v_words, "v_scales": v_scales,
            "prior_sd": prior_sd, "prior_mean": prior_mean, "reliability": reliability}

def reference(responses, a_words, a_scales, half_width, v_words, v_scales, prior_sd, prior_mean, reliability):
    A = unpack4(a_words, a_scales)
    V = unpack4(v_words, v_scales)
    score = mxq(f64(responses), 1, "e4m3") @ A
    ability = np.tanh(score) * f64(half_width)[None, :]
    mixed = mxq(ability, 1, "e4m3") @ V
    y = mixed * f64(prior_sd)[None, :] * f64(reliability)[:, None] + f64(prior_mean)[None, :]
    words, scales = planes(y.T)
    return y, words, scales

@@ -1,0 +1,366 @@
+from contextlib import ExitStack
+
+import concourse.mybir as mybir
+from concourse.masks import make_identity
+
+PERSONS, ITEMS, DIMS, TRAITS = 1280, 2048, 1024, 1536
+FLOPS = 2 * PERSONS * ITEMS * DIMS + 2 * PERSONS * DIMS * TRAITS
+
+F32 = mybir.dt.float32
+BF16 = mybir.dt.bfloat16
+I32 = mybir.dt.int32
+U32 = mybir.dt.uint32
+U8 = mybir.dt.uint8
+FP8X4 = mybir.dt.float8_e4m3fn_x4
+FP4X4 = mybir.dt.float4_e2m1fn_x4
+ALU = mybir.AluOpType
+ACT = mybir.ActivationFunctionType
+
+P = 128
+PASS = 512
+BANK = 512
+BANKS = 8
+TILES = PERSONS // P
+ITEM_PASSES = ITEMS // PASS
+DIM_PASSES = DIMS // PASS
+TRAIT_GROUPS = TRAITS // PASS
+HALVES = 2
+HALF = ITEMS // HALVES
+EARLY_TILES = 7
+
+
+def tile_item_response_traits_h1_kernel(
+    tc, responses, a_words, a_scales, half_width, v_words, v_scales,
+    prior_sd, prior_mean, reliability, out_0, out_1, out_2,
+):
+    nc = tc.nc
+    with ExitStack() as ctx:
+        keep = ctx.enter_context(tc.tile_pool(name="keep", bufs=1))
+        work = ctx.enter_context(tc.tile_pool(name="work", bufs=2))
+        psum = ctx.enter_context(tc.psum_pool(name="psum", bufs=1))
+        ctx.enter_context(tc.manual_schedule())
+
+        banks_taken = []
+
+        def take_bank(dtype=F32, width=BANK):
+            tag = "bank%d" % (len(banks_taken) % BANKS)
+            bank = psum.tile([P, width], dtype, name=tag, tag=tag)
+            banks_taken.append(tag)
+            return bank
+
+        a_plane = keep.tile([P, ITEM_PASSES, DIMS], U8, align_bytes=64)
+        v_plane = keep.tile([P, DIM_PASSES, TRAITS], U8, align_bytes=64)
+        identity = keep.tile([P, P], F32)
+        identity_bf = keep.tile([P, P], BF16)
+        rel_rows = keep.tile([P, P], BF16)
+        nc.vector.memset(a_plane[:].bitcast(I32), 0)
+        nc.gpsimd.memset(rel_rows[:], 0.0)
+        make_identity(nc, identity[:])
+        nc.gpsimd.memset(v_plane[:].bitcast(I32), 0)
+        make_identity(nc, identity_bf[:])
+
+        resp = {}
+
+        def load_responses(i):
+            for h in range(HALVES):
+                t = keep.tile([P, HALF], BF16, name="resp%d_%d" % (i, h), align_bytes=64)
+                nc.sync.dma_start(out=t[:], in_=responses[i * P:(i + 1) * P, h * HALF:(h + 1) * HALF])
+                resp[(i, h)] = t
+
+        def load_scales(plane, scales):
+            for q in range(4):
+                nc.sync.dma_start(
+                    out=plane[32 * q:32 * q + 4, :, :].bitcast(I32),
+                    in_=scales[:, 4 * q:4 * q + 4, :].rearrange("g r n -> r g n").bitcast(I32),
+                )
+
+        def load_row(vec, width, name):
+            t = keep.tile([P, width], BF16, name=name, align_bytes=64)
+            nc.sync.dma_start(out=t[:], in_=vec.partition_broadcast(P))
+            return t
+
+        a_codes = []
+
+        def load_a(c):
+            t = keep.tile([P, ITEM_PASSES, 2 * BANK], U8, name="a_codes%d" % c, align_bytes=64)
+            nc.sync.dma_start(
+                out=t[:].bitcast(I32),
+                in_=a_words[:, :, 2 * BANK * c:2 * BANK * (c + 1)].rearrange("g p n -> p g n").bitcast(I32),
+            )
+            a_codes.append(t)
+
+        load_responses(0)
+        load_scales(a_plane, a_scales)
+        load_a(0)
+        load_a(1)
+        load_responses(1)
+        width_row = load_row(half_width, DIMS, "width_row")
+        nc.sync.dma_start(out=rel_rows[0:TILES, :], in_=reliability.rearrange("(i p) -> i p", p=P))
+        load_responses(2)
+        load_scales(v_plane, v_scales)
+        v_codes = keep.tile([P, DIM_PASSES, 2 * TRAITS], U8, align_bytes=64)
+        nc.sync.dma_start(out=v_codes[:].bitcast(I32), in_=v_words.rearrange("g p n -> p g n").bitcast(I32))
+        sd_row = load_row(prior_sd, TRAITS, "sd_row")
+        mean_row = load_row(prior_mean, TRAITS, "mean_row")
+        for i in range(3, TILES):
+            load_responses(i)
+
+        width_sorted = keep.tile([P, DIMS], BF16, align_bytes=64)
+        rel = keep.tile([P, TILES], F32)
+
+        tiles = {}
+
+        def transpose_responses(i, h):
+            bank = take_bank()
+            words = resp[(i, h)][:].bitcast(F32)
+            for g in range(2):
+                for u in range(2):
+                    j = 2 * g + u
+                    nc.tensor.transpose(bank[:, j * P:(j + 1) * P], words[:, 256 * g + u:256 * (g + 1):2], identity[:])
+            tiles[("resp_bank", i, h)] = bank
+
+        def transpose_sorted(name, i, src, first, count):
+            bank = take_bank()
+            words = src[:].bitcast(F32)
+            for j in range(count):
+                nc.tensor.transpose(bank[:, j * P:(j + 1) * P], words[:, (first + j) * P:(first + j + 1) * P], identity[:])
+            tiles[(name, i, first)] = bank
+
+        def unload_words(bank, dst, first_pass, passes, copy=nc.scalar.copy):
+            words = dst[:].bitcast(F32)[:, 2 * P * first_pass:2 * P * (first_pass + passes)]
+            copy(
+                out=words.rearrange("p (g r u) -> p g r u", g=passes, u=2),
+                in_=bank[:, 0:2 * P * passes].rearrange("p (g u r) -> p g r u", g=passes, u=2),
+            )
+
+        def unload_responses(i, h):
+            t = work.tile([P, HALF], BF16, name="resp_t", tag="resp_t", bufs=4, align_bytes=64)
+            unload_words(tiles[("resp_bank", i, h)], t, 0, 2)
+            tiles[("resp_t", i, h)] = t
+
+        def quantize(src, name, key):
+            codes = work.tile([P, 2 * P], U32, name=name + "_codes", tag=name + "_codes", bufs=6, align_bytes=64)
+            scales = work.tile([P, 2 * P], U8, name=name + "_scales", tag=name + "_scales", bufs=6, align_bytes=64)
+            nc.vector.quantize_mx(out=codes[:].bitcast(FP8X4), scales=scales[:], in_=src[:])
+            tiles[key] = (codes, scales)
+
+        def score_matmuls(i, c):
+            bank = take_bank()
+            for g in range(ITEM_PASSES):
+                codes, scales = tiles[("resp_q", i, g // 2)]
+                cols = slice((g % 2) * P, (g % 2 + 1) * P)
+                nc.tensor.matmul_mx(
+                    out=bank[:], lhsT=codes[:, cols].bitcast(FP8X4), lhsT_scale=scales[:, cols],
+                    rhs=a_codes[c][:, g, :].bitcast(FP4X4), rhs_scale=a_plane[:, g, c * BANK:(c + 1) * BANK],
+                    start=(g == 0), stop=(g == ITEM_PASSES - 1),
+                )
+            tiles[("score", i, c)] = bank
+
+        def logistic(i, c):
+            t = work.tile([P, BANK], F32, name="curve", tag="curve", bufs=4)
+            nc.scalar.activation(
+                out=t[:].rearrange("p (u q e) -> p u q e", u=2, e=2),
+                in_=tiles[("score", i, c)][:].rearrange("p (q u e) -> p u q e", u=2, e=2),
+                func=ACT.Tanh,
+            )
+            tiles[("curve", i, c)] = t
+
+        def stretch(i, c):
+            if c == 0:
+                tiles[("ability", i)] = work.tile([P, DIMS], BF16, name="ability", tag="ability", align_bytes=64)
+            cols = slice(c * BANK, (c + 1) * BANK)
+            nc.vector.tensor_tensor(
+                out=tiles[("ability", i)][:, cols], in0=tiles[("curve", i, c)][:], in1=width_sorted[:, cols], op=ALU.mult)
+
+        def mix_matmuls(i, g):
+            bank = take_bank()
+            codes, scales = tiles[("ability_q", i)]
+            for c in range(DIM_PASSES):
+                cols = slice(c * P, (c + 1) * P)
+                nc.tensor.matmul_mx(
+                    out=bank[:], lhsT=codes[:, cols].bitcast(FP8X4), lhsT_scale=scales[:, cols],
+                    rhs=v_codes[:, c, 2 * BANK * g:2 * BANK * (g + 1)].bitcast(FP4X4),
+                    rhs_scale=v_plane[:, c, g * BANK:(g + 1) * BANK],
+                    start=(c == 0), stop=(c == DIM_PASSES - 1),
+                )
+            tiles[("mixed", i, g)] = bank
+
+        def scale_traits(i, g):
+            if g == 0:
+                tiles[("y", i)] = work.tile([P, TRAITS], F32, name="y", tag="y", bufs=4)
+            cols = slice(g * BANK, (g + 1) * BANK)
+            nc.vector.scalar_tensor_tensor(
+                out=tiles[("y", i)][:, cols], in0=tiles[("mixed", i, g)][:], scalar=rel[:, i:i + 1],
+                in1=sd_row[:, cols], op0=ALU.mult, op1=ALU.mult)
+
+        def add_mean(i, g, engine):
+            cols = slice(g * BANK, (g + 1) * BANK)
+            y = tiles[("y", i)]
+            engine.tensor_tensor(out=y[:, cols], in0=y[:, cols], in1=mean_row[:, cols], op=ALU.add)
+
+        def round_traits(i, g, copy=nc.scalar.copy):
+            if g == 0:
+                tiles[("y_bf", i)] = work.tile([P, TRAITS], BF16, name="y_bf", tag="y_bf", bufs=3, align_bytes=64)
+            cols = slice(g * BANK, (g + 1) * BANK)
+            copy(
+                out=tiles[("y_bf", i)][:, cols].rearrange("p (u q e) -> p u q e", u=2, e=2),
+                in_=tiles[("y", i)][:, cols].rearrange("p (q u e) -> p u q e", u=2, e=2),
+            )
+
+        def scale_group(i):
+            return (0, EARLY_TILES) if i < EARLY_TILES else (EARLY_TILES, TILES)
+
+        def quantize_traits(i, g):
+            first, last = scale_group(i)
+            if g == 0:
+                tiles[("y_codes", i)] = work.tile([P, TRAIT_GROUPS, P], U32, name="y_codes", tag="y_codes", bufs=3, align_bytes=64)
+            if i == first and g == 0:
+                tiles[("y_scales", first)] = keep.tile(
+                    [P, TRAIT_GROUPS, (last - first) * P], U8, name="y_scales%d" % first, align_bytes=64)
+            cols = slice((i - first) * P, (i - first + 1) * P)
+            nc.vector.quantize_mx(
+                out=tiles[("y_codes", i)][:, g, :].bitcast(FP8X4), scales=tiles[("y_scales", first)][:, g, cols],
+                in_=tiles[("y_t", i)][:, g * PASS:(g + 1) * PASS])
+
+        def store_planes(i):
+            nc.sync.dma_start(
+                out=out_1[:, :, i * P:(i + 1) * P, :].rearrange("g p m t -> p g (m t)").bitcast(I32),
+                in_=tiles[("y_codes", i)][:].bitcast(I32))
+            first, last = scale_group(i)
+            if i == last - 1:
+                for q in range(4):
+                    nc.sync.dma_start(
+                        out=out_2[:, 4 * q:4 * q + 4, first * P:last * P].rearrange("g r m -> r g m").bitcast(I32),
+                        in_=tiles[("y_scales", first)][32 * q:32 * q + 4, :, :].bitcast(I32))
+
+        def store_traits(i, first, last):
+            cols = slice(first * BANK, last * BANK)
+            nc.sync.dma_start(out=out_0[i * P:(i + 1) * P, cols], in_=tiles[("y", i)][:, cols])
+
+        def unload_traits(i, first_group, groups, copy=nc.scalar.copy):
+            if first_group == 0:
+                tiles[("y_t", i)] = work.tile([P, TRAITS], BF16, name="y_t", tag="y_t", bufs=3, align_bytes=64)
+            unload_words(tiles[("y_bank", i, 2 * first_group)], tiles[("y_t", i)], first_group, groups, copy)
+
+        def has(i):
+            return 0 <= i < TILES
+
+        for step in range(-1, TILES):
+            now, mix, out, plane = step, step - 1, step - 2, step - 3
+            fresh = {-1: [0], 0: [], 1: [1, 2]}.get(step, [step + 1] if has(step + 1) else [])
+
+            for i in fresh[:1]:
+                for h in range(HALVES):
+                    transpose_responses(i, h)
+            if step == 1:
+                rel_bank = take_bank(BF16, P)
+                nc.tensor.transpose(rel_bank[:], rel_rows[:], identity_bf[:])
+            if has(mix):
+                transpose_sorted("ability_bank", mix, tiles[("ability", mix)], 0, 4)
+            for i in fresh[1:]:
+                for h in range(HALVES):
+                    transpose_responses(i, h)
+            if has(plane):
+                transpose_sorted("y_bank", plane, tiles[("y_bf", plane)], 0, 4)
+                transpose_sorted("y_bank", plane, tiles[("y_bf", plane)], 4, 2)
+
+            for i in fresh[:1]:
+                for h in range(HALVES):
+                    unload_responses(i, h)
+            if has(mix):
+                ability_t = work.tile([P, DIMS], BF16, name="ability_t", tag="ability_t", align_bytes=64)
+                unload_words(tiles[("ability_bank", mix, 0)], ability_t, 0, 2)
+            if step == 1:
+                nc.scalar.copy(out=rel[:], in_=rel_bank[:, 0:TILES])
+            for i in fresh[1:]:
+                for h in range(HALVES):
+                    unload_responses(i, h)
+            if has(plane):
+                unload_traits(plane, 0, 2)
+                unload_traits(plane, 2, 1)
+
+            if step == 1:
+                for h in range(HALVES):
+                    quantize(tiles[("resp_t", 1, h)], "resp", ("resp_q", 1, h))
+            if has(out):
+                scale_traits(out, 0)
+                add_mean(out, 0, nc.gpsimd)
+                scale_traits(out, 1)
+                scale_traits(out, 2)
+                add_mean(out, 1, nc.vector)
+            if has(mix):
+                quantize(ability_t, "ability", ("ability_q", mix))
+            if has(out):
+                add_mean(out, 2, nc.vector)
+                store_traits(out, 0, TRAIT_GROUPS)
+            if has(plane):
+                for g in range(TRAIT_GROUPS):
+                    quantize_traits(plane, g)
+                store_planes(plane)
+            for i in fresh[-1:]:
+                for h in range(HALVES):
+                    quantize(tiles[("resp_t", i, h)], "resp", ("resp_q", i, h))
+
+            if has(now):
+                for c in range(DIM_PASSES):
+                    score_matmuls(now, c)
+            if has(mix):
+                for g in range(TRAIT_GROUPS):
+                    mix_matmuls(mix, g)
+
+            if has(now):
+                logistic(now, 0)
+            if has(out):
+                round_traits(out, 0)
+            if has(now):
+                logistic(now, 1)
+            if has(out):
+                round_traits(out, 1)
+                round_traits(out, 2)
+            if step == 0:
+                nc.vector.tensor_copy(
+                    out=width_sorted[:].bitcast(F32).rearrange("p (c u q) -> p c u q", c=DIM_PASSES, u=2),
+                    in_=width_row[:].bitcast(F32).rearrange("p (c q u) -> p c u q", c=DIM_PASSES, u=2),
+                )
+            if has(now):
+                for c in range(DIM_PASSES):
+                    stretch(now, c)
+
+        last, before, plane = TILES - 1, TILES - 2, TILES - 3
+        groups = range(TRAIT_GROUPS)
+        transpose_sorted("ability_bank", last, tiles[("ability", last)], 0, 4)
+        transpose_sorted("y_bank", plane, tiles[("y_bf", plane)], 0, 4)
+        transpose_sorted("y_bank", plane, tiles[("y_bf", plane)], 4, 2)
+        ability_t = work.tile([P, DIMS], BF16, name="ability_t", tag="ability_t", align_bytes=64)
+        unload_words(tiles[("ability_bank", last, 0)], ability_t, 0, 2)
+        unload_traits(plane, 0, 2)
+        unload_traits(plane, 2, 1)
+        for g in groups:
+            scale_traits(before, g)
+            add_mean(before, g, nc.gpsimd)
+            round_traits(before, g)
+            if g == 1:
+                quantize(ability_t, "ability", ("ability_q", last))
+        store_traits(before, 0, TRAIT_GROUPS)
+        for g in groups:
+            mix_matmuls(last, g)
+        for g in groups:
+            scale_traits(last, g)
+        transpose_sorted("y_bank", before, tiles[("y_bf", before)], 0, 4)
+        transpose_sorted("y_bank", before, tiles[("y_bf", before)], 4, 2)
+        unload_traits(before, 0, 2)
+        unload_traits(before, 2, 1)
+        for g in groups:
+            add_mean(last, g, nc.vector)
+            store_traits(last, g, g + 1)
+            quantize_traits(plane, g)
+            round_traits(last, g, nc.scalar.copy if g == 0 else nc.vector.tensor_copy)
+        store_planes(plane)
+        for g in groups:
+            quantize_traits(before, g)
+        store_planes(before)
+        for g in groups:
+            transpose_sorted("y_bank", last, tiles[("y_bf", last)], 2 * g, 2)
+            unload_traits(last, g, 1)
+            quantize_traits(last, g)
+        store_planes(last)

@@ -54,8 +54,8 @@ def tile_item_response_traits_h1_kernel(
         identity_bf = keep.tile([P, P], BF16)
         rel_rows = keep.tile([P, P], BF16)
         nc.vector.memset(a_plane[:].bitcast(I32), 0)
-        nc.gpsimd.memset(rel_rows[:], 0.0)
         make_identity(nc, identity[:])
+        nc.gpsimd.memset(rel_rows[:], 0.0)
         nc.gpsimd.memset(v_plane[:].bitcast(I32), 0)
         make_identity(nc, identity_bf[:])
 
@@ -74,11 +74,6 @@ def tile_item_response_traits_h1_kernel(
                     in_=scales[:, 4 * q:4 * q + 4, :].rearrange("g r n -> r g n").bitcast(I32),
                 )
 
-        def load_row(vec, width, name):
-            t = keep.tile([P, width], BF16, name=name, align_bytes=64)
-            nc.sync.dma_start(out=t[:], in_=vec.partition_broadcast(P))
-            return t
-
         a_codes = []
 
         def load_a(c):
@@ -89,26 +84,53 @@ def tile_item_response_traits_h1_kernel(
             )
             a_codes.append(t)
 
+        def load_columns(vec, name):
+            run = vec.shape[0] // (2 * P)
+            t = keep.tile([P, 2, 16], BF16, name=name)
+            nc.scalar.dma_start(out=t[:, :, 0:run], in_=vec.rearrange("(h n w) -> n h w", h=2, n=P))
+            return t
+
+        width_cols = load_columns(half_width, "width_cols")
+        sd_cols = load_columns(prior_sd, "sd_cols")
+        mean_cols = load_columns(prior_mean, "mean_cols")
         load_responses(0)
         load_scales(a_plane, a_scales)
         load_a(0)
         load_a(1)
         load_responses(1)
-        width_row = load_row(half_width, DIMS, "width_row")
-        nc.sync.dma_start(out=rel_rows[0:TILES, :], in_=reliability.rearrange("(i p) -> i p", p=P))
         load_responses(2)
+        nc.sync.dma_start(out=rel_rows[0:TILES, :], in_=reliability.rearrange("(i p) -> i p", p=P))
         load_scales(v_plane, v_scales)
         v_codes = keep.tile([P, DIM_PASSES, 2 * TRAITS], U8, align_bytes=64)
         nc.sync.dma_start(out=v_codes[:].bitcast(I32), in_=v_words.rearrange("g p n -> p g n").bitcast(I32))
-        sd_row = load_row(prior_sd, TRAITS, "sd_row")
-        mean_row = load_row(prior_mean, TRAITS, "mean_row")
         for i in range(3, TILES):
             load_responses(i)
 
+        sd_row = keep.tile([P, TRAITS], BF16, align_bytes=64)
+        mean_row = keep.tile([P, TRAITS], BF16, align_bytes=64)
         width_sorted = keep.tile([P, DIMS], BF16, align_bytes=64)
         rel = keep.tile([P, TILES], F32)
 
         tiles = {}
+
+        def spread(cols, pieces):
+            bank = take_bank()
+            words = cols[:].bitcast(F32)
+            for k, (h, j) in enumerate(pieces):
+                nc.tensor.transpose(bank[:, k * P:(k + 1) * P], words[:, h, j:j + 1].to_broadcast([P, P]), identity[:])
+            return bank
+
+        def spread_width():
+            bank = spread(width_cols, [(c, u) for c in range(DIM_PASSES) for u in range(2)])
+            nc.scalar.copy(out=width_sorted[:].bitcast(F32), in_=bank[:])
+
+        def spread_traits(cols, row):
+            for h, copy in enumerate((nc.vector.tensor_copy, nc.scalar.copy)):
+                bank = spread(cols, [(h, j) for j in range(3)])
+                copy(
+                    out=row[:].bitcast(F32)[:, 3 * P * h:3 * P * (h + 1)].rearrange("p (n j) -> p n j", j=3),
+                    in_=bank[:, 0:3 * P].rearrange("p (j n) -> p n j", j=3),
+                )
 
         def transpose_responses(i, h):
             bank = take_bank()
@@ -238,13 +260,24 @@ def tile_item_response_traits_h1_kernel(
             nc.sync.dma_start(out=out_0[i * P:(i + 1) * P, cols], in_=tiles[("y", i)][:, cols])
 
         def unload_traits(i, first_group, groups, copy=nc.scalar.copy):
-            if first_group == 0:
+            if ("y_t", i) not in tiles:
                 tiles[("y_t", i)] = work.tile([P, TRAITS], BF16, name="y_t", tag="y_t", bufs=3, align_bytes=64)
             unload_words(tiles[("y_bank", i, 2 * first_group)], tiles[("y_t", i)], first_group, groups, copy)
 
         def has(i):
             return 0 <= i < TILES
 
+        def transpose_traits(i):
+            transpose_sorted("y_bank", i, tiles[("y_bf", i)], 0, 4)
+            transpose_sorted("y_bank", i, tiles[("y_bf", i)], 4, 2)
+
+        def unload_ability(i):
+            t = work.tile([P, DIMS], BF16, name="ability_t", tag="ability_t", align_bytes=64)
+            unload_words(tiles[("ability_bank", i, 0)], t, 0, 2)
+            tiles[("ability_t", i)] = t
+
+        groups = range(TRAIT_GROUPS)
+        spread_width()
         for step in range(-1, TILES):
             now, mix, out, plane = step, step - 1, step - 2, step - 3
             fresh = {-1: [0], 0: [], 1: [1, 2]}.get(step, [step + 1] if has(step + 1) else [])
@@ -301,6 +334,10 @@ def tile_item_response_traits_h1_kernel(
                 for h in range(HALVES):
                     quantize(tiles[("resp_t", i, h)], "resp", ("resp_q", i, h))
 
+            if step == -1:
+                spread_traits(sd_cols, sd_row)
+                spread_traits(mean_cols, mean_row)
+
             if has(now):
                 for c in range(DIM_PASSES):
                     score_matmuls(now, c)
@@ -317,11 +354,6 @@ def tile_item_response_traits_h1_kernel(
             if has(out):
                 round_traits(out, 1)
                 round_traits(out, 2)
-            if step == 0:
-                nc.vector.tensor_copy(
-                    out=width_sorted[:].bitcast(F32).rearrange("p (c u q) -> p c u q", c=DIM_PASSES, u=2),
-                    in_=width_row[:].bitcast(F32).rearrange("p (c q u) -> p c u q", c=DIM_PASSES, u=2),
-                )
             if has(now):
                 for c in range(DIM_PASSES):
                     stretch(now, c)

@@ -212,13 +212,13 @@ def tile_item_response_traits_h1_kernel(
                 tiles[("y", i)] = work.tile([P, TRAITS], F32, name="y", tag="y", bufs=4)
             cols = slice(g * BANK, (g + 1) * BANK)
             nc.vector.scalar_tensor_tensor(
-                out=tiles[("y", i)][:, cols], in0=tiles[("mixed", i, g)][:], scalar=rel[:, i:i + 1],
-                in1=sd_row[:, cols], op0=ALU.mult, op1=ALU.mult)
+                out=tiles[("y", i)][:, cols], in0=sd_row[:, cols], scalar=rel[:, i:i + 1],
+                in1=tiles[("mixed", i, g)][:], op0=ALU.mult, op1=ALU.mult)
 
-        def add_mean(i, g, engine):
+        def add_mean(i, g):
             cols = slice(g * BANK, (g + 1) * BANK)
             y = tiles[("y", i)]
-            engine.tensor_tensor(out=y[:, cols], in0=y[:, cols], in1=mean_row[:, cols], op=ALU.add)
+            nc.vector.tensor_tensor(out=y[:, cols], in0=y[:, cols], in1=mean_row[:, cols], op=ALU.add)
 
         def round_traits(i, g, copy=nc.scalar.copy):
             if g == 0:
@@ -282,6 +282,9 @@ def tile_item_response_traits_h1_kernel(
             now, mix, out, plane = step, step - 1, step - 2, step - 3
             fresh = {-1: [0], 0: [], 1: [1, 2]}.get(step, [step + 1] if has(step + 1) else [])
 
+            if has(mix) and fresh:
+                stretch(mix, 1)
+
             for i in fresh[:1]:
                 for h in range(HALVES):
                     transpose_responses(i, h)
@@ -316,16 +319,14 @@ def tile_item_response_traits_h1_kernel(
                 for h in range(HALVES):
                     quantize(tiles[("resp_t", 1, h)], "resp", ("resp_q", 1, h))
             if has(out):
-                scale_traits(out, 0)
-                add_mean(out, 0, nc.gpsimd)
                 scale_traits(out, 1)
+                add_mean(out, 0)
                 scale_traits(out, 2)
-                add_mean(out, 1, nc.vector)
+                add_mean(out, 1)
+                add_mean(out, 2)
+                store_traits(out, 0, TRAIT_GROUPS)
             if has(mix):
                 quantize(ability_t, "ability", ("ability_q", mix))
-            if has(out):
-                add_mean(out, 2, nc.vector)
-                store_traits(out, 0, TRAIT_GROUPS)
             if has(plane):
                 for g in range(TRAIT_GROUPS):
                     quantize_traits(plane, g)
@@ -355,8 +356,11 @@ def tile_item_response_traits_h1_kernel(
                 round_traits(out, 1)
                 round_traits(out, 2)
             if has(now):
-                for c in range(DIM_PASSES):
-                    stretch(now, c)
+                stretch(now, 0)
+            if has(now) and not has(step + 2):
+                stretch(now, 1)
+            if has(mix):
+                scale_traits(mix, 0)
 
         last, before, plane = TILES - 1, TILES - 2, TILES - 3
         groups = range(TRAIT_GROUPS)
@@ -367,32 +371,43 @@ def tile_item_response_traits_h1_kernel(
         unload_words(tiles[("ability_bank", last, 0)], ability_t, 0, 2)
         unload_traits(plane, 0, 2)
         unload_traits(plane, 2, 1)
-        for g in groups:
-            scale_traits(before, g)
-            add_mean(before, g, nc.gpsimd)
-            round_traits(before, g)
-            if g == 1:
-                quantize(ability_t, "ability", ("ability_q", last))
-        store_traits(before, 0, TRAIT_GROUPS)
+        scale_traits(before, 1)
+        add_mean(before, 0)
+        quantize(ability_t, "ability", ("ability_q", last))
+        scale_traits(before, 2)
+        add_mean(before, 1)
         for g in groups:
             mix_matmuls(last, g)
+        quantize_traits(plane, 0)
+        add_mean(before, 2)
+        store_traits(before, 0, TRAIT_GROUPS)
         for g in groups:
-            scale_traits(last, g)
+            round_traits(before, g)
         transpose_sorted("y_bank", before, tiles[("y_bf", before)], 0, 4)
         transpose_sorted("y_bank", before, tiles[("y_bf", before)], 4, 2)
-        unload_traits(before, 0, 2)
-        unload_traits(before, 2, 1)
-        for g in groups:
-            add_mean(last, g, nc.vector)
-            store_traits(last, g, g + 1)
-            quantize_traits(plane, g)
-            round_traits(last, g, nc.scalar.copy if g == 0 else nc.vector.tensor_copy)
+        scale_traits(last, 0)
+        scale_traits(last, 1)
+        add_mean(last, 0)
+        store_traits(last, 0, 1)
+        scale_traits(last, 2)
+        add_mean(last, 1)
+        store_traits(last, 1, 2)
+        quantize_traits(plane, 1)
+        add_mean(last, 2)
+        store_traits(last, 2, 3)
+        quantize_traits(plane, 2)
         store_planes(plane)
+        unload_traits(before, 0, 2)
+        round_traits(last, 0)
+        unload_traits(before, 2, 1)
+        round_traits(last, 1)
+        round_traits(last, 2)
         for g in groups:
             quantize_traits(before, g)
         store_planes(before)
         for g in groups:
             transpose_sorted("y_bank", last, tiles[("y_bf", last)], 2 * g, 2)
-            unload_traits(last, g, 1)
+            unload_traits(last, g, 1, nc.vector.tensor_copy if g < 2 else nc.scalar.copy)
+        for g in groups:
             quantize_traits(last, g)
         store_planes(last)

@@ -27,6 +27,7 @@ TRAIT_GROUPS = TRAITS // PASS
 HALVES = 2
 HALF = ITEMS // HALVES
 EARLY_TILES = 7
+SORTED_HALF = 0
 
 
 def tile_item_response_traits_h1_kernel(
@@ -96,8 +97,8 @@ def tile_item_response_traits_h1_kernel(
         load_responses(0)
         load_scales(a_plane, a_scales)
         load_a(0)
-        load_a(1)
         load_responses(1)
+        load_a(1)
         load_responses(2)
         nc.sync.dma_start(out=rel_rows[0:TILES, :], in_=reliability.rearrange("(i p) -> i p", p=P))
         load_scales(v_plane, v_scales)
@@ -132,13 +133,24 @@ def tile_item_response_traits_h1_kernel(
                     in_=bank[:, 0:3 * P].rearrange("p (j n) -> p n j", j=3),
                 )
 
+        def sort_responses(i):
+            t = work.tile([P, HALF // 2], F32, name="resp_sorted", tag="resp_sorted")
+            nc.scalar.copy(
+                out=t[:].rearrange("p (g u q) -> p g q u", g=2, u=2),
+                in_=resp[(i, SORTED_HALF)][:].bitcast(F32).rearrange("p (g q u) -> p g q u", g=2, u=2),
+            )
+            tiles[("resp_sorted", i)] = t
+
         def transpose_responses(i, h):
             bank = take_bank()
-            words = resp[(i, h)][:].bitcast(F32)
             for g in range(2):
                 for u in range(2):
                     j = 2 * g + u
-                    nc.tensor.transpose(bank[:, j * P:(j + 1) * P], words[:, 256 * g + u:256 * (g + 1):2], identity[:])
+                    if h == SORTED_HALF and ("resp_sorted", i) in tiles:
+                        words = tiles[("resp_sorted", i)][:, j * P:(j + 1) * P]
+                    else:
+                        words = resp[(i, h)][:].bitcast(F32)[:, 256 * g + u:256 * (g + 1):2]
+                    nc.tensor.transpose(bank[:, j * P:(j + 1) * P], words, identity[:])
             tiles[("resp_bank", i, h)] = bank
 
         def transpose_sorted(name, i, src, first, count):
@@ -276,91 +288,93 @@ def tile_item_response_traits_h1_kernel(
             unload_words(tiles[("ability_bank", i, 0)], t, 0, 2)
             tiles[("ability_t", i)] = t
 
+        def turn_responses(i):
+            for h in range(HALVES):
+                transpose_responses(i, h)
+            for h in range(HALVES):
+                unload_responses(i, h)
+
+        def quantize_responses(i, h):
+            quantize(tiles[("resp_t", i, h)], "resp", ("resp_q", i, h))
+
         groups = range(TRAIT_GROUPS)
         spread_width()
-        for step in range(-1, TILES):
-            now, mix, out, plane = step, step - 1, step - 2, step - 3
-            fresh = {-1: [0], 0: [], 1: [1, 2]}.get(step, [step + 1] if has(step + 1) else [])
+        turn_responses(0)
+        quantize_responses(0, 0)
+        quantize_responses(0, 1)
+        spread_traits(sd_cols, sd_row)
+        spread_traits(mean_cols, mean_row)
+        score_matmuls(0, 0)
+        logistic(0, 0)
+        turn_responses(1)
+        stretch(0, 0)
+        quantize_responses(1, 0)
+        score_matmuls(0, 1)
+        logistic(0, 1)
+        quantize_responses(1, 1)
+        stretch(0, 1)
+        turn_responses(2)
+        score_matmuls(1, 0)
+        transpose_sorted("ability_bank", 0, tiles[("ability", 0)], 0, 4)
+        rel_bank = take_bank(BF16, P)
+        nc.tensor.transpose(rel_bank[:], rel_rows[:], identity_bf[:])
+        unload_ability(0)
+        nc.scalar.copy(out=rel[:], in_=rel_bank[:, 0:TILES])
+        quantize_responses(2, 0)
+        quantize(tiles[("ability_t", 0)], "ability", ("ability_q", 0))
+        logistic(1, 0)
+        stretch(1, 0)
+        score_matmuls(1, 1)
+        logistic(1, 1)
+        sort_responses(3)
+        stretch(1, 1)
+        for g in groups:
+            mix_matmuls(0, g)
+        scale_traits(0, 0)
 
-            if has(mix) and fresh:
-                stretch(mix, 1)
+        for now in range(2, TILES):
+            ahead, mix, out, plane = now + 1, now - 1, now - 2, now - 3
 
-            for i in fresh[:1]:
-                for h in range(HALVES):
-                    transpose_responses(i, h)
-            if step == 1:
-                rel_bank = take_bank(BF16, P)
-                nc.tensor.transpose(rel_bank[:], rel_rows[:], identity_bf[:])
-            if has(mix):
-                transpose_sorted("ability_bank", mix, tiles[("ability", mix)], 0, 4)
-            for i in fresh[1:]:
-                for h in range(HALVES):
-                    transpose_responses(i, h)
+            transpose_sorted("ability_bank", mix, tiles[("ability", mix)], 0, 4)
             if has(plane):
-                transpose_sorted("y_bank", plane, tiles[("y_bf", plane)], 0, 4)
-                transpose_sorted("y_bank", plane, tiles[("y_bf", plane)], 4, 2)
-
-            for i in fresh[:1]:
-                for h in range(HALVES):
-                    unload_responses(i, h)
-            if has(mix):
-                ability_t = work.tile([P, DIMS], BF16, name="ability_t", tag="ability_t", align_bytes=64)
-                unload_words(tiles[("ability_bank", mix, 0)], ability_t, 0, 2)
-            if step == 1:
-                nc.scalar.copy(out=rel[:], in_=rel_bank[:, 0:TILES])
-            for i in fresh[1:]:
-                for h in range(HALVES):
-                    unload_responses(i, h)
+                transpose_traits(plane)
+            unload_ability(mix)
             if has(plane):
                 unload_traits(plane, 0, 2)
                 unload_traits(plane, 2, 1)
 
-            if step == 1:
-                for h in range(HALVES):
-                    quantize(tiles[("resp_t", 1, h)], "resp", ("resp_q", 1, h))
+            quantize_responses(now, 1)
             if has(out):
                 scale_traits(out, 1)
                 add_mean(out, 0)
                 scale_traits(out, 2)
+            quantize(tiles[("ability_t", mix)], "ability", ("ability_q", mix))
+            if has(out):
                 add_mean(out, 1)
                 add_mean(out, 2)
                 store_traits(out, 0, TRAIT_GROUPS)
-            if has(mix):
-                quantize(ability_t, "ability", ("ability_q", mix))
             if has(plane):
-                for g in range(TRAIT_GROUPS):
+                for g in groups:
                     quantize_traits(plane, g)
                 store_planes(plane)
-            for i in fresh[-1:]:
-                for h in range(HALVES):
-                    quantize(tiles[("resp_t", i, h)], "resp", ("resp_q", i, h))
 
-            if step == -1:
-                spread_traits(sd_cols, sd_row)
-                spread_traits(mean_cols, mean_row)
-
-            if has(now):
-                for c in range(DIM_PASSES):
-                    score_matmuls(now, c)
-            if has(mix):
-                for g in range(TRAIT_GROUPS):
-                    mix_matmuls(mix, g)
-
-            if has(now):
-                logistic(now, 0)
+            for c in range(DIM_PASSES):
+                score_matmuls(now, c)
+                if has(out):
+                    round_traits(out, c)
+                logistic(now, c)
+                stretch(now, c)
+            if has(ahead):
+                turn_responses(ahead)
             if has(out):
-                round_traits(out, 0)
-            if has(now):
-                logistic(now, 1)
-            if has(out):
-                round_traits(out, 1)
                 round_traits(out, 2)
-            if has(now):
-                stretch(now, 0)
-            if has(now) and not has(step + 2):
-                stretch(now, 1)
-            if has(mix):
-                scale_traits(mix, 0)
+            if has(ahead + 1):
+                sort_responses(ahead + 1)
+            if has(ahead):
+                quantize_responses(ahead, 0)
+            for g in groups:
+                mix_matmuls(mix, g)
+            scale_traits(mix, 0)
 
         last, before, plane = TILES - 1, TILES - 2, TILES - 3
         groups = range(TRAIT_GROUPS)
@@ -392,22 +406,21 @@ def tile_item_response_traits_h1_kernel(
         scale_traits(last, 2)
         add_mean(last, 1)
         store_traits(last, 1, 2)
-        quantize_traits(plane, 1)
         add_mean(last, 2)
         store_traits(last, 2, 3)
-        quantize_traits(plane, 2)
-        store_planes(plane)
         unload_traits(before, 0, 2)
         round_traits(last, 0)
         unload_traits(before, 2, 1)
         round_traits(last, 1)
-        round_traits(last, 2)
+        quantize_traits(plane, 1)
+        round_traits(last, 2, nc.vector.tensor_copy)
+        quantize_traits(plane, 2)
+        store_planes(plane)
         for g in groups:
             quantize_traits(before, g)
         store_planes(before)
         for g in groups:
             transpose_sorted("y_bank", last, tiles[("y_bf", last)], 2 * g, 2)
-            unload_traits(last, g, 1, nc.vector.tensor_copy if g < 2 else nc.scalar.copy)
-        for g in groups:
+            unload_traits(last, g, 1, nc.scalar.copy)
             quantize_traits(last, g)
         store_planes(last)

from contextlib import ExitStack

import concourse.mybir as mybir
from concourse.masks import make_identity

PERSONS, ITEMS, DIMS, TRAITS = 1280, 2048, 1024, 1536
FLOPS = 2 * PERSONS * ITEMS * DIMS + 2 * PERSONS * DIMS * TRAITS

F32 = mybir.dt.float32
BF16 = mybir.dt.bfloat16
I32 = mybir.dt.int32
U32 = mybir.dt.uint32
U8 = mybir.dt.uint8
FP8X4 = mybir.dt.float8_e4m3fn_x4
FP4X4 = mybir.dt.float4_e2m1fn_x4
ALU = mybir.AluOpType
ACT = mybir.ActivationFunctionType

P = 128
PASS = 512
BANK = 512
BANKS = 8
TILES = PERSONS // P
ITEM_PASSES = ITEMS // PASS
DIM_PASSES = DIMS // PASS
TRAIT_GROUPS = TRAITS // PASS
HALVES = 2
HALF = ITEMS // HALVES
EARLY_TILES = 7
SORTED_HALF = 0


def tile_item_response_traits_h1_kernel(
    tc, responses, a_words, a_scales, half_width, v_words, v_scales,
    prior_sd, prior_mean, reliability, out_0, out_1, out_2,
):
    nc = tc.nc
    with ExitStack() as ctx:
        keep = ctx.enter_context(tc.tile_pool(name="keep", bufs=1))
        work = ctx.enter_context(tc.tile_pool(name="work", bufs=2))
        psum = ctx.enter_context(tc.psum_pool(name="psum", bufs=1))
        ctx.enter_context(tc.manual_schedule())

        banks_taken = []

        def take_bank(dtype=F32, width=BANK):
            tag = "bank%d" % (len(banks_taken) % BANKS)
            bank = psum.tile([P, width], dtype, name=tag, tag=tag)
            banks_taken.append(tag)
            return bank

        a_plane = keep.tile([P, ITEM_PASSES, DIMS], U8, align_bytes=64)
        v_plane = keep.tile([P, DIM_PASSES, TRAITS], U8, align_bytes=64)
        identity = keep.tile([P, P], F32)
        identity_bf = keep.tile([P, P], BF16)
        rel_rows = keep.tile([P, P], BF16)
        nc.vector.memset(a_plane[:].bitcast(I32), 0)
        make_identity(nc, identity[:])
        nc.gpsimd.memset(rel_rows[:], 0.0)
        nc.gpsimd.memset(v_plane[:].bitcast(I32), 0)
        make_identity(nc, identity_bf[:])

        resp = {}

        def load_responses(i):
            for h in range(HALVES):
                t = keep.tile([P, HALF], BF16, name="resp%d_%d" % (i, h), align_bytes=64)
                nc.sync.dma_start(out=t[:], in_=responses[i * P:(i + 1) * P, h * HALF:(h + 1) * HALF])
                resp[(i, h)] = t

        def load_scales(plane, scales):
            for q in range(4):
                nc.sync.dma_start(
                    out=plane[32 * q:32 * q + 4, :, :].bitcast(I32),
                    in_=scales[:, 4 * q:4 * q + 4, :].rearrange("g r n -> r g n").bitcast(I32),
                )

        a_codes = []

        def load_a(c):
            t = keep.tile([P, ITEM_PASSES, 2 * BANK], U8, name="a_codes%d" % c, align_bytes=64)
            nc.sync.dma_start(
                out=t[:].bitcast(I32),
                in_=a_words[:, :, 2 * BANK * c:2 * BANK * (c + 1)].rearrange("g p n -> p g n").bitcast(I32),
            )
            a_codes.append(t)

        def load_columns(vec, name):
            run = vec.shape[0] // (2 * P)
            t = keep.tile([P, 2, 16], BF16, name=name)
            nc.scalar.dma_start(out=t[:, :, 0:run], in_=vec.rearrange("(h n w) -> n h w", h=2, n=P))
            return t

        width_cols = load_columns(half_width, "width_cols")
        sd_cols = load_columns(prior_sd, "sd_cols")
        mean_cols = load_columns(prior_mean, "mean_cols")
        load_responses(0)
        load_scales(a_plane, a_scales)
        load_a(0)
        load_responses(1)
        load_a(1)
        load_responses(2)
        nc.sync.dma_start(out=rel_rows[0:TILES, :], in_=reliability.rearrange("(i p) -> i p", p=P))
        load_scales(v_plane, v_scales)
        v_codes = keep.tile([P, DIM_PASSES, 2 * TRAITS], U8, align_bytes=64)
        nc.sync.dma_start(out=v_codes[:].bitcast(I32), in_=v_words.rearrange("g p n -> p g n").bitcast(I32))
        for i in range(3, TILES):
            load_responses(i)

        sd_row = keep.tile([P, TRAITS], BF16, align_bytes=64)
        mean_row = keep.tile([P, TRAITS], BF16, align_bytes=64)
        width_sorted = keep.tile([P, DIMS], BF16, align_bytes=64)
        rel = keep.tile([P, TILES], F32)

        tiles = {}

        def spread(cols, pieces):
            bank = take_bank()
            words = cols[:].bitcast(F32)
            for k, (h, j) in enumerate(pieces):
                nc.tensor.transpose(bank[:, k * P:(k + 1) * P], words[:, h, j:j + 1].to_broadcast([P, P]), identity[:])
            return bank

        def spread_width():
            bank = spread(width_cols, [(c, u) for c in range(DIM_PASSES) for u in range(2)])
            nc.scalar.copy(out=width_sorted[:].bitcast(F32), in_=bank[:])

        def spread_traits(cols, row):
            for h, copy in enumerate((nc.vector.tensor_copy, nc.scalar.copy)):
                bank = spread(cols, [(h, j) for j in range(3)])
                copy(
                    out=row[:].bitcast(F32)[:, 3 * P * h:3 * P * (h + 1)].rearrange("p (n j) -> p n j", j=3),
                    in_=bank[:, 0:3 * P].rearrange("p (j n) -> p n j", j=3),
                )

        def sort_responses(i):
            t = work.tile([P, HALF // 2], F32, name="resp_sorted", tag="resp_sorted")
            nc.scalar.copy(
                out=t[:].rearrange("p (g u q) -> p g q u", g=2, u=2),
                in_=resp[(i, SORTED_HALF)][:].bitcast(F32).rearrange("p (g q u) -> p g q u", g=2, u=2),
            )
            tiles[("resp_sorted", i)] = t

        def transpose_responses(i, h):
            bank = take_bank()
            for g in range(2):
                for u in range(2):
                    j = 2 * g + u
                    if h == SORTED_HALF and ("resp_sorted", i) in tiles:
                        words = tiles[("resp_sorted", i)][:, j * P:(j + 1) * P]
                    else:
                        words = resp[(i, h)][:].bitcast(F32)[:, 256 * g + u:256 * (g + 1):2]
                    nc.tensor.transpose(bank[:, j * P:(j + 1) * P], words, identity[:])
            tiles[("resp_bank", i, h)] = bank

        def transpose_sorted(name, i, src, first, count):
            bank = take_bank()
            words = src[:].bitcast(F32)
            for j in range(count):
                nc.tensor.transpose(bank[:, j * P:(j + 1) * P], words[:, (first + j) * P:(first + j + 1) * P], identity[:])
            tiles[(name, i, first)] = bank

        def unload_words(bank, dst, first_pass, passes, copy=nc.scalar.copy):
            words = dst[:].bitcast(F32)[:, 2 * P * first_pass:2 * P * (first_pass + passes)]
            copy(
                out=words.rearrange("p (g r u) -> p g r u", g=passes, u=2),
                in_=bank[:, 0:2 * P * passes].rearrange("p (g u r) -> p g r u", g=passes, u=2),
            )

        def unload_responses(i, h):
            t = work.tile([P, HALF], BF16, name="resp_t", tag="resp_t", bufs=4, align_bytes=64)
            unload_words(tiles[("resp_bank", i, h)], t, 0, 2)
            tiles[("resp_t", i, h)] = t

        def quantize(src, name, key):
            codes = work.tile([P, 2 * P], U32, name=name + "_codes", tag=name + "_codes", bufs=6, align_bytes=64)
            scales = work.tile([P, 2 * P], U8, name=name + "_scales", tag=name + "_scales", bufs=6, align_bytes=64)
            nc.vector.quantize_mx(out=codes[:].bitcast(FP8X4), scales=scales[:], in_=src[:])
            tiles[key] = (codes, scales)

        def score_matmuls(i, c):
            bank = take_bank()
            for g in range(ITEM_PASSES):
                codes, scales = tiles[("resp_q", i, g // 2)]
                cols = slice((g % 2) * P, (g % 2 + 1) * P)
                nc.tensor.matmul_mx(
                    out=bank[:], lhsT=codes[:, cols].bitcast(FP8X4), lhsT_scale=scales[:, cols],
                    rhs=a_codes[c][:, g, :].bitcast(FP4X4), rhs_scale=a_plane[:, g, c * BANK:(c + 1) * BANK],
                    start=(g == 0), stop=(g == ITEM_PASSES - 1),
                )
            tiles[("score", i, c)] = bank

        def logistic(i, c):
            t = work.tile([P, BANK], F32, name="curve", tag="curve", bufs=4)
            nc.scalar.activation(
                out=t[:].rearrange("p (u q e) -> p u q e", u=2, e=2),
                in_=tiles[("score", i, c)][:].rearrange("p (q u e) -> p u q e", u=2, e=2),
                func=ACT.Tanh,
            )
            tiles[("curve", i, c)] = t

        def stretch(i, c):
            if c == 0:
                tiles[("ability", i)] = work.tile([P, DIMS], BF16, name="ability", tag="ability", align_bytes=64)
            cols = slice(c * BANK, (c + 1) * BANK)
            nc.vector.tensor_tensor(
                out=tiles[("ability", i)][:, cols], in0=tiles[("curve", i, c)][:], in1=width_sorted[:, cols], op=ALU.mult)

        def mix_matmuls(i, g):
            bank = take_bank()
            codes, scales = tiles[("ability_q", i)]
            for c in range(DIM_PASSES):
                cols = slice(c * P, (c + 1) * P)
                nc.tensor.matmul_mx(
                    out=bank[:], lhsT=codes[:, cols].bitcast(FP8X4), lhsT_scale=scales[:, cols],
                    rhs=v_codes[:, c, 2 * BANK * g:2 * BANK * (g + 1)].bitcast(FP4X4),
                    rhs_scale=v_plane[:, c, g * BANK:(g + 1) * BANK],
                    start=(c == 0), stop=(c == DIM_PASSES - 1),
                )
            tiles[("mixed", i, g)] = bank

        def scale_traits(i, g):
            if g == 0:
                tiles[("y", i)] = work.tile([P, TRAITS], F32, name="y", tag="y", bufs=4)
            cols = slice(g * BANK, (g + 1) * BANK)
            nc.vector.scalar_tensor_tensor(
                out=tiles[("y", i)][:, cols], in0=sd_row[:, cols], scalar=rel[:, i:i + 1],
                in1=tiles[("mixed", i, g)][:], op0=ALU.mult, op1=ALU.mult)

        def add_mean(i, g):
            cols = slice(g * BANK, (g + 1) * BANK)
            y = tiles[("y", i)]
            nc.vector.tensor_tensor(out=y[:, cols], in0=y[:, cols], in1=mean_row[:, cols], op=ALU.add)

        def round_traits(i, g, copy=nc.scalar.copy):
            if g == 0:
                tiles[("y_bf", i)] = work.tile([P, TRAITS], BF16, name="y_bf", tag="y_bf", bufs=3, align_bytes=64)
            cols = slice(g * BANK, (g + 1) * BANK)
            copy(
                out=tiles[("y_bf", i)][:, cols].rearrange("p (u q e) -> p u q e", u=2, e=2),
                in_=tiles[("y", i)][:, cols].rearrange("p (q u e) -> p u q e", u=2, e=2),
            )

        def scale_group(i):
            return (0, EARLY_TILES) if i < EARLY_TILES else (EARLY_TILES, TILES)

        def quantize_traits(i, g):
            first, last = scale_group(i)
            if g == 0:
                tiles[("y_codes", i)] = work.tile([P, TRAIT_GROUPS, P], U32, name="y_codes", tag="y_codes", bufs=3, align_bytes=64)
            if i == first and g == 0:
                tiles[("y_scales", first)] = keep.tile(
                    [P, TRAIT_GROUPS, (last - first) * P], U8, name="y_scales%d" % first, align_bytes=64)
            cols = slice((i - first) * P, (i - first + 1) * P)
            nc.vector.quantize_mx(
                out=tiles[("y_codes", i)][:, g, :].bitcast(FP8X4), scales=tiles[("y_scales", first)][:, g, cols],
                in_=tiles[("y_t", i)][:, g * PASS:(g + 1) * PASS])

        def store_planes(i):
            nc.sync.dma_start(
                out=out_1[:, :, i * P:(i + 1) * P, :].rearrange("g p m t -> p g (m t)").bitcast(I32),
                in_=tiles[("y_codes", i)][:].bitcast(I32))
            first, last = scale_group(i)
            if i == last - 1:
                for q in range(4):
                    nc.sync.dma_start(
                        out=out_2[:, 4 * q:4 * q + 4, first * P:last * P].rearrange("g r m -> r g m").bitcast(I32),
                        in_=tiles[("y_scales", first)][32 * q:32 * q + 4, :, :].bitcast(I32))

        def store_traits(i, first, last):
            cols = slice(first * BANK, last * BANK)
            nc.sync.dma_start(out=out_0[i * P:(i + 1) * P, cols], in_=tiles[("y", i)][:, cols])

        def unload_traits(i, first_group, groups, copy=nc.scalar.copy):
            if ("y_t", i) not in tiles:
                tiles[("y_t", i)] = work.tile([P, TRAITS], BF16, name="y_t", tag="y_t", bufs=3, align_bytes=64)
            unload_words(tiles[("y_bank", i, 2 * first_group)], tiles[("y_t", i)], first_group, groups, copy)

        def has(i):
            return 0 <= i < TILES

        def transpose_traits(i):
            transpose_sorted("y_bank", i, tiles[("y_bf", i)], 0, 4)
            transpose_sorted("y_bank", i, tiles[("y_bf", i)], 4, 2)

        def unload_ability(i):
            t = work.tile([P, DIMS], BF16, name="ability_t", tag="ability_t", align_bytes=64)
            unload_words(tiles[("ability_bank", i, 0)], t, 0, 2)
            tiles[("ability_t", i)] = t

        def turn_responses(i):
            for h in range(HALVES):
                transpose_responses(i, h)
            for h in range(HALVES):
                unload_responses(i, h)

        def quantize_responses(i, h):
            quantize(tiles[("resp_t", i, h)], "resp", ("resp_q", i, h))

        groups = range(TRAIT_GROUPS)
        spread_width()
        turn_responses(0)
        quantize_responses(0, 0)
        quantize_responses(0, 1)
        spread_traits(sd_cols, sd_row)
        spread_traits(mean_cols, mean_row)
        score_matmuls(0, 0)
        logistic(0, 0)
        turn_responses(1)
        stretch(0, 0)
        quantize_responses(1, 0)
        score_matmuls(0, 1)
        logistic(0, 1)
        quantize_responses(1, 1)
        stretch(0, 1)
        turn_responses(2)
        score_matmuls(1, 0)
        transpose_sorted("ability_bank", 0, tiles[("ability", 0)], 0, 4)
        rel_bank = take_bank(BF16, P)
        nc.tensor.transpose(rel_bank[:], rel_rows[:], identity_bf[:])
        unload_ability(0)
        nc.scalar.copy(out=rel[:], in_=rel_bank[:, 0:TILES])
        quantize_responses(2, 0)
        quantize(tiles[("ability_t", 0)], "ability", ("ability_q", 0))
        logistic(1, 0)
        stretch(1, 0)
        score_matmuls(1, 1)
        logistic(1, 1)
        sort_responses(3)
        stretch(1, 1)
        for g in groups:
            mix_matmuls(0, g)
        scale_traits(0, 0)

        for now in range(2, TILES):
            ahead, mix, out, plane = now + 1, now - 1, now - 2, now - 3

            transpose_sorted("ability_bank", mix, tiles[("ability", mix)], 0, 4)
            if has(plane):
                transpose_traits(plane)
            unload_ability(mix)
            if has(plane):
                unload_traits(plane, 0, 2)
                unload_traits(plane, 2, 1)

            quantize_responses(now, 1)
            if has(out):
                scale_traits(out, 1)
                add_mean(out, 0)
                scale_traits(out, 2)
            quantize(tiles[("ability_t", mix)], "ability", ("ability_q", mix))
            if has(out):
                add_mean(out, 1)
                add_mean(out, 2)
                store_traits(out, 0, TRAIT_GROUPS)
            if has(plane):
                for g in groups:
                    quantize_traits(plane, g)
                store_planes(plane)

            for c in range(DIM_PASSES):
                score_matmuls(now, c)
                if has(out):
                    round_traits(out, c)
                logistic(now, c)
                stretch(now, c)
            if has(ahead):
                turn_responses(ahead)
            if has(out):
                round_traits(out, 2)
            if has(ahead + 1):
                sort_responses(ahead + 1)
            if has(ahead):
                quantize_responses(ahead, 0)
            for g in groups:
                mix_matmuls(mix, g)
            scale_traits(mix, 0)

        last, before, plane = TILES - 1, TILES - 2, TILES - 3
        groups = range(TRAIT_GROUPS)
        transpose_sorted("ability_bank", last, tiles[("ability", last)], 0, 4)
        transpose_sorted("y_bank", plane, tiles[("y_bf", plane)], 0, 4)
        transpose_sorted("y_bank", plane, tiles[("y_bf", plane)], 4, 2)
        ability_t = work.tile([P, DIMS], BF16, name="ability_t", tag="ability_t", align_bytes=64)
        unload_words(tiles[("ability_bank", last, 0)], ability_t, 0, 2)
        unload_traits(plane, 0, 2)
        unload_traits(plane, 2, 1)
        scale_traits(before, 1)
        add_mean(before, 0)
        quantize(ability_t, "ability", ("ability_q", last))
        scale_traits(before, 2)
        add_mean(before, 1)
        for g in groups:
            mix_matmuls(last, g)
        quantize_traits(plane, 0)
        add_mean(before, 2)
        store_traits(before, 0, TRAIT_GROUPS)
        for g in groups:
            round_traits(before, g)
        transpose_sorted("y_bank", before, tiles[("y_bf", before)], 0, 4)
        transpose_sorted("y_bank", before, tiles[("y_bf", before)], 4, 2)
        scale_traits(last, 0)
        scale_traits(last, 1)
        add_mean(last, 0)
        store_traits(last, 0, 1)
        scale_traits(last, 2)
        add_mean(last, 1)
        store_traits(last, 1, 2)
        add_mean(last, 2)
        store_traits(last, 2, 3)
        unload_traits(before, 0, 2)
        round_traits(last, 0)
        unload_traits(before, 2, 1)
        round_traits(last, 1)
        quantize_traits(plane, 1)
        round_traits(last, 2, nc.vector.tensor_copy)
        quantize_traits(plane, 2)
        store_planes(plane)
        for g in groups:
            quantize_traits(before, g)
        store_planes(before)
        for g in groups:
            transpose_sorted("y_bank", last, tiles[("y_bf", last)], 2 * g, 2)
            unload_traits(last, g, 1, nc.scalar.copy)
            quantize_traits(last, g)
        store_planes(last)
